import numpy as np
import ml_dtypes


def mxq(x, axis, fmt="e4m3"):
    dtype, down = {"e4m3": (ml_dtypes.float8_e4m3fn, 7), "e5m2": (ml_dtypes.float8_e5m2, 14)}[fmt]
    v = np.moveaxis(np.asarray(x, np.float32).astype(ml_dtypes.bfloat16).astype(np.float64), axis, -1)
    blocks = v.reshape(v.shape[:-1] + (-1, 32))
    amax = np.abs(blocks).max(-1, keepdims=True)
    byte = np.maximum(np.where(amax > 0, np.frexp(amax)[1] - 1 + 127, 0) - down, 1)
    scale = np.exp2(byte - 127.0)
    codes = (blocks / scale).astype(np.float32).astype(dtype).astype(np.float64)
    return np.moveaxis((codes * scale).reshape(v.shape), -1, axis)


WIDE = False


def mx_kscale(k):
    if not WIDE:
        return np.ones(k)
    levels = np.array([10, -10, 5, -5, 0])
    if k % 512:
        return np.exp2(np.random.permutation(np.resize(levels, k // 32))).repeat(32)
    a = np.empty((k // 512, 16))
    for p in range(k // 512):
        a[p, :8] = np.random.permutation(np.resize(levels, 8))
        for g in range(8):
            far = levels[np.abs(levels - a[p, g]) >= 10]
            a[p, g + 8] = far[np.random.randint(len(far))]
    return np.exp2(a.ravel()).repeat(32)


def f64(x):
    return np.asarray(x).astype(np.float64)


def striped(idx):
    return np.tile(idx.reshape(-1, 16).T, (8, 1)).astype(np.uint16)


def unstriped(offs):
    return offs[:16].T.reshape(-1).astype(np.int64)


E2M1 = np.array([0.0, 0.5, 1.0, 1.5, 2.0, 3.0, 4.0, 6.0, -0.0, -0.5, -1.0, -1.5, -2.0, -3.0, -4.0, -6.0])


def pack_weight(w, fmt):
    k, n = w.shape
    w = f64(np.asarray(w, np.float32).astype(ml_dtypes.bfloat16)).reshape(k // 32, 32, n)
    amax = np.abs(w).max(1)
    if fmt == "e4m3":
        byte = np.frexp(amax)[1] - 1 + 127 - 7
    else:
        mant, ex = np.frexp(amax / 6.0)
        byte = np.where(mant > 0.5, ex, ex - 1) + 127
    byte = np.clip(np.where(amax > 0, byte, 1), 1, 254)
    scaled = (w * np.exp2(127.0 - byte)[:, None, :]).reshape(k, n).astype(np.float32)
    by_word = np.ascontiguousarray(scaled.reshape(k // 512, 128, 4, n).transpose(0, 1, 3, 2))
    if fmt == "e4m3":
        words = by_word.astype(ml_dtypes.float8_e4m3fn).view(np.uint8)
    else:
        c = by_word.astype(ml_dtypes.float4_e2m1fn).view(np.uint8) & 0xF
        words = (c[..., 0::2] | (c[..., 1::2] << 4)).reshape(k // 512, 128, 2 * n)
    return np.ascontiguousarray(words), np.ascontiguousarray(byte.astype(np.uint8).reshape(k // 512, 16, n))


def unpack_weight(words, scales, fmt):
    g, _, n = scales.shape
    words = np.ascontiguousarray(words).reshape(g, 128, n, -1)
    if fmt == "e4m3":
        vals = words.view(ml_dtypes.float8_e4m3fn).astype(np.float64)
    else:
        nib = np.empty((g, 128, n, 4), np.uint8)
        nib[..., 0::2] = words & 0xF
        nib[..., 1::2] = words >> 4
        vals = E2M1[nib]
    vals = vals * np.repeat(np.exp2(scales.astype(np.float64) - 127.0), 8, axis=1)[..., None]
    return vals.transpose(0, 1, 3, 2).reshape(g * 512, n)


def gelu(v):
    return 0.5 * v * (1.0 + np.tanh(np.sqrt(2.0 / np.pi) * (v + 0.044715 * v**3)))


K, T, S, S2 = 1024, 2048, 1024, 512


def setup_inputs():
    n = np.random.standard_normal
    s = mx_kscale(K)[:, None]
    d = {}
    d["tab_words"], d["tab_scales"] = pack_weight(n((K, T)) * s, "e4m3")
    d["offs"] = striped(np.random.permutation(T)[:S])
    d["offs2"] = striped(np.random.permutation(T)[:S2])
    d["w1"] = (1.5 * n((K, K)) / s / s.T / K).astype(np.float32)
    d["w4_words"], d["w4_scales"] = pack_weight(n((K, S)) / s / K ** 0.5, "e2m1")
    d["gain"] = (0.7 * np.exp(0.3 * n(S2))).astype(np.float32)
    return d


def reference(tab_words, tab_scales, offs, offs2, w1, w4_words, w4_scales, gain):
    tw = unpack_weight(tab_words, tab_scales, "e4m3")
    v = tw[:, unstriped(offs)]
    v2 = tw[:, unstriped(offs2)]
    w4 = unpack_weight(w4_words, w4_scales, "e2m1")
    h = np.maximum(mxq(f64(w1), 0, "e4m3").T @ v, 0.0)
    e = v2.T @ mxq(h, 0, "e4m3")
    f = v2.T @ w4
    return np.maximum(e, f) + f64(gain)[:, None] * e

@@ -1,0 +1,310 @@
+from contextlib import ExitStack
+
+import concourse.mybir as mybir
+
+K, T, S, S2 = 1024, 2048, 1024, 512
+FLOPS = 2 * K * K * S + 2 * 2 * K * S2 * S
+
+F32 = mybir.dt.float32
+BF16 = mybir.dt.bfloat16
+I32 = mybir.dt.int32
+U32 = mybir.dt.uint32
+U16 = mybir.dt.uint16
+U8 = mybir.dt.uint8
+FP8X4 = mybir.dt.float8_e4m3fn_x4
+FP4X4 = mybir.dt.float4_e2m1fn_x4
+ACT = mybir.ActivationFunctionType
+ALU = mybir.AluOpType
+
+P = 128
+PACK = 4
+KP = P * PACK
+PASSES = K // KP
+HALF = 512
+NH = S // HALF
+MT = S2 // P
+FTAG, ETAG, HTAG = "acc", "acc", "acc"
+BUFS = {"acc": 8}
+
+
+def tile_list_shard_fit_scores_kernel(tc, tab_words, tab_scales, offs, offs2, w1, w4_words, w4_scales, gain, out):
+    nc = tc.nc
+    with ExitStack() as ctx:
+        keep = ctx.enter_context(tc.tile_pool(name="keep", bufs=1))
+        ring = ctx.enter_context(tc.tile_pool(name="ring", bufs=4))
+        psum = ctx.enter_context(tc.psum_pool(name="psum", bufs=4))
+
+        def held(shape, dtype, name):
+            return keep.tile(shape, dtype, name=name, align_bytes=64)
+
+        idx = keep.tile([P, S // 16], U16, name="idx")
+        idx2 = keep.tile([P, S2 // 16], U16, name="idx2")
+        nc.sync.dma_start(idx2[:], offs2)
+        nc.sync.dma_start(idx[:], offs)
+
+        tab_sc = held([P, T], U8, "tab_sc")
+        nc.gpsimd.memset(tab_sc[:, : 5 * T // 8].bitcast(I32), 0)
+        nc.vector.memset(tab_sc[:, 5 * T // 8 :].bitcast(I32), 0)
+        w4_sc = held([P, PASSES, S], U8, "w4_sc")
+        nc.vector.memset(w4_sc[:].rearrange("p a n -> p (a n)").bitcast(I32), 0)
+        v2_sc1 = held([P, S2], U8, "v2_sc1")
+        nc.vector.memset(v2_sc1[:].bitcast(I32), 0)
+
+        tab_w = [held([P, T], I32, "tab_w%d" % a) for a in range(PASSES)]
+        w1_raw = {}
+        w4_w = held([P, PASSES, 2 * S], U8, "w4_w")
+        gain_sb = held([P, MT], F32, "gain_sb")
+
+        def load_tab(a):
+            nc.sync.dma_start(tab_w[a][:], tab_words[a].rearrange("p t i -> p (t i)").bitcast(I32))
+
+        def load_w1(b, a, m0, m1, tag=None):
+            raw = keep.tile([P, PACK, PACK * (m1 - m0)], F32, name="w1_raw%d%d_%d" % (b, a, m0), tag=tag or "w1_raw%d%d_%d" % (b, a, m0), align_bytes=64)
+            w1_raw[b, a, m0] = raw
+            nc.sync.dma_start(
+                raw[:],
+                w1[KP * a : KP * (a + 1), KP * b + PACK * m0 : KP * b + PACK * m1].rearrange("(p t) c -> p t c", t=PACK),
+            )
+
+        with nc.allow_non_contiguous_dma(reason="one gain for each partition and row tile"):
+            nc.sync.dma_start(gain_sb[:], gain.rearrange("(c p) -> p c", p=P))
+        load_w1(0, 0, 0, P // 2)
+        for q in range(4):
+            nc.sync.dma_start(
+                tab_sc[32 * q : 32 * q + 8, :].bitcast(I32),
+                tab_scales[:, 4 * q : 4 * q + 4, :].bitcast(I32),
+            )
+        v2_sc = held([P, S2], U8, "v2_sc")
+        nc.vector.tensor_copy(v2_sc[:], tab_sc[:].indirect(idx2[:]))
+        nc.sync.dma_start(v2_sc1[0 : P - 4, :].bitcast(I32), v2_sc[4:P, :].bitcast(I32))
+        warm = keep.tile([P, 2], F32, name="warm")
+        nc.gpsimd.memset(warm[:, 0:1], 0.0)
+        nc.scalar.activation(warm[:, 1:2], warm[:, 0:1], ACT.Relu)
+        load_tab(0)
+        load_w1(0, 0, P // 2, P)
+        load_tab(1)
+        for q in range(4):
+            nc.sync.dma_start(
+                w4_sc[32 * q : 32 * q + 4, :, :].bitcast(I32),
+                w4_scales[:, 4 * q : 4 * q + 4, :].rearrange("a r n -> r a n").bitcast(I32),
+            )
+        load_w1(0, 1, 0, P // 2)
+        load_w1(0, 1, P // 2, P, "then_f0")
+        nc.sync.dma_start(w4_w[:].bitcast(I32), w4_words.rearrange("a p n -> p a n").bitcast(I32))
+        load_w1(1, 0, 0, P)
+        load_w1(1, 1, 0, P // 2)
+        load_w1(1, 1, P // 2, P)
+
+        v2_w = [held([P, S2], U32, "v2_w%d" % a) for a in range(PASSES)]
+        v_sc, v_w = {}, {}
+
+        def half(jh):
+            return idx[:, jh * (HALF // 16) : (jh + 1) * (HALF // 16)]
+
+        def gather_v_sc(jh, tag):
+            v_sc[jh] = keep.tile([P, HALF], U8, name="v_sc%d" % jh, tag=tag, align_bytes=64)
+            nc.vector.tensor_copy(v_sc[jh][:], tab_sc[:].indirect(half(jh)))
+
+        def gather_v(a, jh, tag):
+            v_w[a, jh] = keep.tile([P, HALF], U32, name="v_w%d%d" % (a, jh), tag=tag, align_bytes=64)
+            nc.vector.tensor_copy(v_w[a, jh][:], tab_w[a][:].bitcast(U32).indirect(half(jh)))
+
+        def gather_v2(a):
+            nc.vector.tensor_copy(v2_w[a][:], tab_w[a][:].bitcast(U32).indirect(idx2[:]))
+
+        w1_bf, w1_w, w1_sc = {}, {}, {}
+        for b in range(PASSES):
+            for a in range(PASSES):
+                w1_bf[b, a] = held([P, PACK, P, PACK], BF16, "w1_bf%d%d" % (b, a))
+                w1_w[b, a] = held([P, KP], U32, "w1_w%d%d" % (b, a))
+                w1_sc[b, a] = held([P, KP], U8, "w1_sc%d%d" % (b, a))
+
+        def cast_w1(b, a, m0, m1, on_vector):
+            dst = w1_bf[b, a][:, :, m0:m1, :].rearrange("p u m t -> p m t u")
+            src = w1_raw[b, a, m0][:].rearrange("p t (m u) -> p m t u", u=PACK)
+            if on_vector:
+                nc.vector.tensor_copy(dst, src)
+            else:
+                nc.scalar.activation(dst, src, ACT.Copy)
+
+        def quant_w1(b, a):
+            nc.vector.quantize_mx(
+                out=w1_w[b, a][:].bitcast(FP8X4),
+                scales=w1_sc[b, a][:],
+                in_=w1_bf[b, a][:].rearrange("p u m t -> p (u m t)"),
+            )
+
+        h_bf, h_w, h_sc = {}, {}, {}
+        for b in range(PASSES):
+            for jh in range(NH):
+                h_bf[b, jh] = held([P, HALF, PACK], BF16, "h_bf%d%d" % (b, jh))
+                h_w[b, jh] = held([P, HALF], U32, "h_w%d%d" % (b, jh))
+                h_sc[b, jh] = held([P, HALF], U8, "h_sc%d%d" % (b, jh))
+
+        h_acc = {}
+
+        def h_pass(b, jh, c, a):
+            if a == 0:
+                h_acc[b, jh, c] = psum.tile([P, PACK, P], F32, name="h_acc", tag=HTAG, bufs=BUFS[HTAG])
+            acc = h_acc[b, jh, c]
+            cols = slice(P * c, P * (c + 1))
+            for u in range(PACK):
+                rows = slice(P * u, P * (u + 1))
+                nc.tensor.matmul_mx(
+                    out=acc[:, u, :],
+                    lhsT=w1_w[b, a][:, rows].bitcast(FP8X4),
+                    lhsT_scale=w1_sc[b, a][:, rows],
+                    rhs=v_w[a, jh][:, cols].bitcast(FP8X4),
+                    rhs_scale=v_sc[jh][4 * a :, cols],
+                    start=(a == 0 and u == 0),
+                    stop=(a == PASSES - 1 and u == PACK - 1),
+                )
+
+        def h_relu(b, jh, c, on_vector):
+            dst = h_bf[b, jh][:, P * c : P * (c + 1), :]
+            src = h_acc[b, jh, c][:].rearrange("p u j -> p j u")
+            if on_vector:
+                nc.vector.tensor_scalar(dst, src, 0.0, None, ALU.max)
+            else:
+                nc.scalar.activation(dst, src, ACT.Relu)
+
+        def quant_h(b, jh):
+            nc.vector.quantize_mx(
+                out=h_w[b, jh][:].bitcast(FP8X4),
+                scales=h_sc[b, jh][:],
+                in_=h_bf[b, jh][:].rearrange("p j u -> p (j u)"),
+            )
+
+        f_sb = {}
+
+        def f_tile(jh, mt, on_vector):
+            if mt == 0:
+                f_sb[jh] = keep.tile([P, MT, HALF], F32, name="f_sb%d" % jh, tag="then_f%d" % jh, align_bytes=64)
+            acc = psum.tile([P, HALF], F32, name="f_acc", tag=FTAG, bufs=BUFS[FTAG])
+            rows = slice(P * mt, P * (mt + 1))
+            for a in range(PASSES):
+                nc.tensor.matmul_mx(
+                    out=acc[:],
+                    lhsT=v2_w[a][:, rows].bitcast(FP8X4),
+                    lhsT_scale=(v2_sc, v2_sc1)[a][:, rows],
+                    rhs=w4_w[:, a, 2 * HALF * jh : 2 * HALF * (jh + 1)].bitcast(FP4X4),
+                    rhs_scale=w4_sc[:, a, HALF * jh : HALF * (jh + 1)],
+                    start=(a == 0),
+                    stop=(a == PASSES - 1),
+                )
+            if on_vector:
+                nc.vector.tensor_copy(f_sb[jh][:, mt, :], acc[:])
+            else:
+                nc.scalar.activation(f_sb[jh][:, mt, :], acc[:], ACT.Copy)
+
+        def e_tile(jh, mt, shared):
+            acc = psum.tile([P, HALF], F32, name="e_acc", tag=ETAG, bufs=BUFS[ETAG])
+            rows = slice(P * mt, P * (mt + 1))
+            for b in range(PASSES):
+                nc.tensor.matmul_mx(
+                    out=acc[:],
+                    lhsT=v2_w[b][:, rows].bitcast(FP8X4),
+                    lhsT_scale=(v2_sc, v2_sc1)[b][:, rows],
+                    rhs=h_w[b, jh][:].bitcast(FP8X4),
+                    rhs_scale=h_sc[b, jh][:],
+                    start=(b == 0),
+                    stop=(b == PASSES - 1),
+                )
+            best = ring.tile([P, HALF], F32, name="best")
+            nc.vector.tensor_tensor(best[:], acc[:], f_sb[jh][:, mt, :], ALU.max)
+            res = ring.tile([P, HALF], F32, name="res")
+            if shared:
+                again = ring.tile([P, HALF], F32, name="again")
+                nc.scalar.activation(again[:], acc[:], ACT.Copy, scale=gain_sb[:, mt : mt + 1])
+                nc.gpsimd.tensor_tensor(res[:], best[:], again[:], ALU.add)
+            else:
+                nc.vector.scalar_tensor_tensor(res[:], acc[:], gain_sb[:, mt : mt + 1], best[:], ALU.mult, ALU.add)
+            nc.sync.dma_start(out[rows, HALF * jh : HALF * (jh + 1)], res[:])
+
+        cast_w1(0, 0, 0, P // 2, False)
+        gather_v_sc(0, "v_sc0")
+        gather_v_sc(1, "v_sc1")
+        gather_v2(0)
+        gather_v(0, 0, "v_w00")
+        cast_w1(0, 0, P // 2, P, False)
+        quant_w1(0, 0)
+        gather_v(1, 0, "v_w10")
+        gather_v2(1)
+        cast_w1(0, 1, 0, P // 2, False)
+        cast_w1(0, 1, P // 2, P, False)
+        h_pass(0, 0, 0, 0)
+        h_pass(0, 0, 1, 0)
+        h_pass(0, 0, 2, 0)
+        h_pass(0, 0, 3, 0)
+        quant_w1(0, 1)
+        gather_v(0, 1, "w1_bf01")
+        gather_v(1, 1, "w1_raw01_0")
+        h_pass(0, 0, 0, 1)
+        h_relu(0, 0, 0, False)
+        h_pass(0, 0, 1, 1)
+        h_relu(0, 0, 1, False)
+        h_pass(0, 0, 2, 1)
+        h_relu(0, 0, 2, False)
+        h_pass(0, 0, 3, 1)
+        h_relu(0, 0, 3, False)
+        f_tile(0, 0, False)
+        f_tile(0, 1, False)
+        f_tile(0, 2, False)
+        f_tile(0, 3, False)
+        cast_w1(1, 0, 0, P, True)
+        quant_w1(1, 0)
+        h_pass(0, 1, 0, 0)
+        h_pass(0, 1, 0, 1)
+        h_relu(0, 1, 0, False)
+        h_pass(0, 1, 1, 0)
+        h_pass(0, 1, 1, 1)
+        h_relu(0, 1, 1, False)
+        h_pass(0, 1, 2, 0)
+        h_pass(0, 1, 2, 1)
+        h_relu(0, 1, 2, False)
+        h_pass(0, 1, 3, 0)
+        h_pass(0, 1, 3, 1)
+        h_relu(0, 1, 3, False)
+        h_pass(1, 0, 0, 0)
+        h_pass(1, 0, 1, 0)
+        h_pass(1, 0, 2, 0)
+        h_pass(1, 0, 3, 0)
+        cast_w1(1, 1, 0, P // 2, True)
+        cast_w1(1, 1, P // 2, P, True)
+        quant_w1(1, 1)
+        quant_h(0, 0)
+        h_pass(1, 0, 0, 1)
+        h_relu(1, 0, 0, False)
+        h_pass(1, 0, 1, 1)
+        h_relu(1, 0, 1, True)
+        h_pass(1, 0, 2, 1)
+        h_relu(1, 0, 2, False)
+        h_pass(1, 0, 3, 1)
+        h_relu(1, 0, 3, True)
+        quant_h(1, 0)
+        quant_h(0, 1)
+        h_pass(1, 1, 0, 0)
+        h_pass(1, 1, 0, 1)
+        h_relu(1, 1, 0, False)
+        h_pass(1, 1, 1, 0)
+        h_pass(1, 1, 1, 1)
+        h_relu(1, 1, 1, False)
+        e_tile(0, 0, False)
+        h_pass(1, 1, 2, 0)
+        h_pass(1, 1, 2, 1)
+        h_relu(1, 1, 2, False)
+        e_tile(0, 1, False)
+        h_pass(1, 1, 3, 0)
+        h_pass(1, 1, 3, 1)
+        h_relu(1, 1, 3, False)
+        quant_h(1, 1)
+        f_tile(1, 0, False)
+        e_tile(0, 2, False)
+        f_tile(1, 1, False)
+        e_tile(0, 3, False)
+        f_tile(1, 2, False)
+        e_tile(1, 0, False)
+        f_tile(1, 3, False)
+        e_tile(1, 1, False)
+        e_tile(1, 2, False)
+        e_tile(1, 3, False)

@@ -66,36 +66,19 @@ def tile_list_shard_fit_scores_kernel(tc, tab_words, tab_scales, offs, offs2, w1
                 w1[KP * a : KP * (a + 1), KP * b + PACK * m0 : KP * b + PACK * m1].rearrange("(p t) c -> p t c", t=PACK),
             )
 
-        with nc.allow_non_contiguous_dma(reason="one gain for each partition and row tile"):
-            nc.sync.dma_start(gain_sb[:], gain.rearrange("(c p) -> p c", p=P))
-        load_w1(0, 0, 0, P // 2)
-        for q in range(4):
-            nc.sync.dma_start(
-                tab_sc[32 * q : 32 * q + 8, :].bitcast(I32),
-                tab_scales[:, 4 * q : 4 * q + 4, :].bitcast(I32),
-            )
-        v2_sc = held([P, S2], U8, "v2_sc")
-        nc.vector.tensor_copy(v2_sc[:], tab_sc[:].indirect(idx2[:]))
-        nc.sync.dma_start(v2_sc1[0 : P - 4, :].bitcast(I32), v2_sc[4:P, :].bitcast(I32))
+        for q in (0, 2, 1, 3):
+            nc.sync.dma_start(tab_sc[32 * q : 32 * q + 8, :].bitcast(I32), tab_scales[:, 4 * q : 4 * q + 4, :].bitcast(I32))
         warm = keep.tile([P, 2], F32, name="warm")
         nc.gpsimd.memset(warm[:, 0:1], 0.0)
         nc.scalar.activation(warm[:, 1:2], warm[:, 0:1], ACT.Relu)
         load_tab(0)
-        load_w1(0, 0, P // 2, P)
+        load_w1(0, 0, 0, P)
+        load_w1(0, 1, 0, P)
         load_tab(1)
-        for q in range(4):
-            nc.sync.dma_start(
-                w4_sc[32 * q : 32 * q + 4, :, :].bitcast(I32),
-                w4_scales[:, 4 * q : 4 * q + 4, :].rearrange("a r n -> r a n").bitcast(I32),
-            )
-        load_w1(0, 1, 0, P // 2)
-        load_w1(0, 1, P // 2, P, "then_f0")
-        nc.sync.dma_start(w4_w[:].bitcast(I32), w4_words.rearrange("a p n -> p a n").bitcast(I32))
         load_w1(1, 0, 0, P)
-        load_w1(1, 1, 0, P // 2)
-        load_w1(1, 1, P // 2, P)
+        load_w1(1, 1, 0, P)
 
-        v2_w = [held([P, S2], U32, "v2_w%d" % a) for a in range(PASSES)]
+        v2_w = {}
         v_sc, v_w = {}, {}
 
         def half(jh):
@@ -109,7 +92,8 @@ def tile_list_shard_fit_scores_kernel(tc, tab_words, tab_scales, offs, offs2, w1
             v_w[a, jh] = keep.tile([P, HALF], U32, name="v_w%d%d" % (a, jh), tag=tag, align_bytes=64)
             nc.vector.tensor_copy(v_w[a, jh][:], tab_w[a][:].bitcast(U32).indirect(half(jh)))
 
-        def gather_v2(a):
+        def gather_v2(a, tag):
+            v2_w[a] = keep.tile([P, S2], U32, name="v2_w%d" % a, tag=tag, align_bytes=64)
             nc.vector.tensor_copy(v2_w[a][:], tab_w[a][:].bitcast(U32).indirect(idx2[:]))
 
         w1_bf, w1_w, w1_sc = {}, {}, {}
@@ -119,11 +103,13 @@ def tile_list_shard_fit_scores_kernel(tc, tab_words, tab_scales, offs, offs2, w1
                 w1_w[b, a] = held([P, KP], U32, "w1_w%d%d" % (b, a))
                 w1_sc[b, a] = held([P, KP], U8, "w1_sc%d%d" % (b, a))
 
-        def cast_w1(b, a, m0, m1, on_vector):
+        def cast_w1(b, a, m0, m1, engine):
             dst = w1_bf[b, a][:, :, m0:m1, :].rearrange("p u m t -> p m t u")
-            src = w1_raw[b, a, m0][:].rearrange("p t (m u) -> p m t u", u=PACK)
-            if on_vector:
+            src = w1_raw[b, a, 0][:, :, PACK * m0 : PACK * m1].rearrange("p t (m u) -> p m t u", u=PACK)
+            if engine == "v":
                 nc.vector.tensor_copy(dst, src)
+            elif engine == "g":
+                nc.gpsimd.tensor_scalar(dst, src, 1.0, 0.0, ALU.mult, ALU.add)
             else:
                 nc.scalar.activation(dst, src, ACT.Copy)
 
@@ -138,7 +124,6 @@ def tile_list_shard_fit_scores_kernel(tc, tab_words, tab_scales, offs, offs2, w1
         for b in range(PASSES):
             for jh in range(NH):
                 h_bf[b, jh] = held([P, HALF, PACK], BF16, "h_bf%d%d" % (b, jh))
-                h_w[b, jh] = held([P, HALF], U32, "h_w%d%d" % (b, jh))
                 h_sc[b, jh] = held([P, HALF], U8, "h_sc%d%d" % (b, jh))
 
         h_acc = {}
@@ -168,11 +153,13 @@ def tile_list_shard_fit_scores_kernel(tc, tab_words, tab_scales, offs, offs2, w1
             else:
                 nc.scalar.activation(dst, src, ACT.Relu)
 
-        def quant_h(b, jh):
+        def quant_h(b, jh, tag, j0=0, j1=HALF):
+            if j0 == 0:
+                h_w[b, jh] = keep.tile([P, HALF], U32, name="h_w%d%d" % (b, jh), tag=tag, align_bytes=64)
             nc.vector.quantize_mx(
-                out=h_w[b, jh][:].bitcast(FP8X4),
-                scales=h_sc[b, jh][:],
-                in_=h_bf[b, jh][:].rearrange("p j u -> p (j u)"),
+                out=h_w[b, jh][:, j0:j1].bitcast(FP8X4),
+                scales=h_sc[b, jh][:, j0:j1],
+                in_=h_bf[b, jh][:, j0:j1, :].rearrange("p j u -> p (j u)"),
             )
 
         f_sb = {}
@@ -221,24 +208,68 @@ def tile_list_shard_fit_scores_kernel(tc, tab_words, tab_scales, offs, offs2, w1
                 nc.vector.scalar_tensor_tensor(res[:], acc[:], gain_sb[:, mt : mt + 1], best[:], ALU.mult, ALU.add)
             nc.sync.dma_start(out[rows, HALF * jh : HALF * (jh + 1)], res[:])
 
-        cast_w1(0, 0, 0, P // 2, False)
-        gather_v_sc(0, "v_sc0")
-        gather_v_sc(1, "v_sc1")
-        gather_v2(0)
+        def e_pair(jh, jq, mp, shared):
+            acc = psum.tile([P, 2, HALF // 2], F32, name="e2_acc", tag=ETAG, bufs=BUFS[ETAG])
+            cols = slice(jq * (HALF // 2), (jq + 1) * (HALF // 2))
+            for i in range(2):
+                rows = slice(P * (2 * mp + i), P * (2 * mp + i + 1))
+                for b in range(PASSES):
+                    nc.tensor.matmul_mx(
+                        out=acc[:, i, :],
+                        lhsT=v2_w[b][:, rows].bitcast(FP8X4),
+                        lhsT_scale=(v2_sc, v2_sc1)[b][:, rows],
+                        rhs=h_w[b, jh][:, cols].bitcast(FP8X4),
+                        rhs_scale=h_sc[b, jh][:, cols],
+                        start=(b == 0),
+                        stop=(b == PASSES - 1),
+                    )
+            best = ring.tile([P, 2, HALF // 2], F32, name="best")
+            nc.vector.tensor_tensor(best[:], acc[:], f_sb[jh][:, 2 * mp : 2 * mp + 2, cols], ALU.max)
+            res = ring.tile([P, 2, HALF // 2], F32, name="res")
+            if shared:
+                again = ring.tile([P, 2, HALF // 2], F32, name="again")
+                for i in range(2):
+                    mt = 2 * mp + i
+                    nc.scalar.activation(again[:, i, :], acc[:, i, :], ACT.Copy, scale=gain_sb[:, mt : mt + 1])
+                nc.gpsimd.tensor_tensor(res[:], best[:], again[:], ALU.add)
+            else:
+                for i in range(2):
+                    mt = 2 * mp + i
+                    nc.vector.scalar_tensor_tensor(res[:, i, :], acc[:, i, :], gain_sb[:, mt : mt + 1], best[:, i, :], ALU.mult, ALU.add)
+            j0 = HALF * jh + cols.start
+            nc.sync.dma_start(out[2 * P * mp : 2 * P * (mp + 1), j0 : j0 + HALF // 2].rearrange("(i p) j -> p i j", p=P), res[:])
+
         gather_v(0, 0, "v_w00")
-        cast_w1(0, 0, P // 2, P, False)
+        gather_v(0, 1, "v_w01")
+        gather_v2(0, "v2_w0")
+        gather_v_sc(0, "v_sc0")
+        v2_sc = keep.tile([P, S2], U8, name="v2_sc", tag="v2_sc", align_bytes=64)
+        nc.vector.tensor_copy(v2_sc[:], tab_sc[:].indirect(idx2[:]))
+        nc.sync.dma_start(v2_sc1[0 : P - 4, :].bitcast(I32), v2_sc[4:P, :].bitcast(I32))
+        for q in (0, 2, 1, 3):
+            nc.sync.dma_start(w4_sc[32 * q : 32 * q + 4, :, :].bitcast(I32), w4_scales[:, 4 * q : 4 * q + 4, :].rearrange("a r n -> r a n").bitcast(I32))
+        nc.sync.dma_start(w4_w[:].bitcast(I32), w4_words.rearrange("a p n -> p a n").bitcast(I32))
+        with nc.allow_non_contiguous_dma(reason="one gain for each partition and row tile"):
+            nc.sync.dma_start(gain_sb[:], gain.rearrange("(c p) -> p c", p=P))
+        cast_w1(0, 0, 0, P // 2, "s")
+        cast_w1(0, 0, P // 2, P, "s")
         quant_w1(0, 0)
-        gather_v(1, 0, "v_w10")
-        gather_v2(1)
-        cast_w1(0, 1, 0, P // 2, False)
-        cast_w1(0, 1, P // 2, P, False)
+        gather_v_sc(1, "w1_bf00")
+        cast_w1(0, 1, 0, P // 2, "s")
+        cast_w1(0, 1, P // 2, P, "s")
         h_pass(0, 0, 0, 0)
         h_pass(0, 0, 1, 0)
         h_pass(0, 0, 2, 0)
         h_pass(0, 0, 3, 0)
+        h_pass(0, 1, 0, 0)
+        h_pass(0, 1, 1, 0)
+        h_pass(0, 1, 2, 0)
+        h_pass(0, 1, 3, 0)
+        gather_v(1, 0, "v_w10")
         quant_w1(0, 1)
-        gather_v(0, 1, "w1_bf01")
-        gather_v(1, 1, "w1_raw01_0")
+        gather_v(1, 1, "w1_bf01")
+        cast_w1(1, 0, 0, P // 2, "v")
+        cast_w1(1, 0, P // 2, P, "s")
         h_pass(0, 0, 0, 1)
         h_relu(0, 0, 0, False)
         h_pass(0, 0, 1, 1)
@@ -247,64 +278,60 @@ def tile_list_shard_fit_scores_kernel(tc, tab_words, tab_scales, offs, offs2, w1
         h_relu(0, 0, 2, False)
         h_pass(0, 0, 3, 1)
         h_relu(0, 0, 3, False)
-        f_tile(0, 0, False)
-        f_tile(0, 1, False)
-        f_tile(0, 2, False)
-        f_tile(0, 3, False)
-        cast_w1(1, 0, 0, P, True)
-        quant_w1(1, 0)
-        h_pass(0, 1, 0, 0)
         h_pass(0, 1, 0, 1)
         h_relu(0, 1, 0, False)
-        h_pass(0, 1, 1, 0)
         h_pass(0, 1, 1, 1)
         h_relu(0, 1, 1, False)
-        h_pass(0, 1, 2, 0)
         h_pass(0, 1, 2, 1)
         h_relu(0, 1, 2, False)
-        h_pass(0, 1, 3, 0)
         h_pass(0, 1, 3, 1)
         h_relu(0, 1, 3, False)
+        quant_w1(1, 0)
+        cast_w1(1, 1, 0, P // 2, "v")
+        cast_w1(1, 1, P // 2, P, "v")
         h_pass(1, 0, 0, 0)
         h_pass(1, 0, 1, 0)
         h_pass(1, 0, 2, 0)
         h_pass(1, 0, 3, 0)
-        cast_w1(1, 1, 0, P // 2, True)
-        cast_w1(1, 1, P // 2, P, True)
+        h_pass(1, 1, 0, 0)
+        h_pass(1, 1, 1, 0)
+        h_pass(1, 1, 2, 0)
+        h_pass(1, 1, 3, 0)
         quant_w1(1, 1)
-        quant_h(0, 0)
+        gather_v2(1, "w1_bf11")
+        quant_h(0, 0, "h_w00")
+        quant_h(0, 1, "h_bf00")
         h_pass(1, 0, 0, 1)
         h_relu(1, 0, 0, False)
         h_pass(1, 0, 1, 1)
-        h_relu(1, 0, 1, True)
+        h_relu(1, 0, 1, False)
         h_pass(1, 0, 2, 1)
-        h_relu(1, 0, 2, False)
+        h_relu(1, 0, 2, True)
         h_pass(1, 0, 3, 1)
-        h_relu(1, 0, 3, True)
-        quant_h(1, 0)
-        quant_h(0, 1)
-        h_pass(1, 1, 0, 0)
+        h_relu(1, 0, 3, False)
+        quant_h(1, 0, "h_w10")
+        f_tile(0, 0, False)
+        f_tile(0, 1, False)
+        e_tile(0, 0, False)
         h_pass(1, 1, 0, 1)
         h_relu(1, 1, 0, False)
-        h_pass(1, 1, 1, 0)
+        e_tile(0, 1, False)
         h_pass(1, 1, 1, 1)
         h_relu(1, 1, 1, False)
-        e_tile(0, 0, False)
-        h_pass(1, 1, 2, 0)
         h_pass(1, 1, 2, 1)
         h_relu(1, 1, 2, False)
-        e_tile(0, 1, False)
-        h_pass(1, 1, 3, 0)
         h_pass(1, 1, 3, 1)
         h_relu(1, 1, 3, False)
-        quant_h(1, 1)
-        f_tile(1, 0, False)
+        quant_h(1, 1, "h_w11")
+        f_tile(0, 2, False)
         e_tile(0, 2, False)
-        f_tile(1, 1, False)
+        f_tile(0, 3, False)
         e_tile(0, 3, False)
-        f_tile(1, 2, False)
+        f_tile(1, 0, False)
         e_tile(1, 0, False)
-        f_tile(1, 3, False)
+        f_tile(1, 1, False)
         e_tile(1, 1, False)
+        f_tile(1, 2, False)
         e_tile(1, 2, False)
+        f_tile(1, 3, False)
         e_tile(1, 3, False)

@@ -104,8 +104,9 @@ def tile_list_shard_fit_scores_kernel(tc, tab_words, tab_scales, offs, offs2, w1
                 w1_sc[b, a] = held([P, KP], U8, "w1_sc%d%d" % (b, a))
 
         def cast_w1(b, a, m0, m1, engine):
-            dst = w1_bf[b, a][:, :, m0:m1, :].rearrange("p u m t -> p m t u")
-            src = w1_raw[b, a, 0][:, :, PACK * m0 : PACK * m1].rearrange("p t (m u) -> p m t u", u=PACK)
+            u0, u1 = m0 // 32, m1 // 32
+            dst = w1_bf[b, a][:, u0:u1, :, :].rearrange("p u m t -> p m t u")
+            src = w1_raw[b, a, 0][:].rearrange("p t (m u) -> p m t u", u=PACK)[:, :, :, u0:u1]
             if engine == "v":
                 nc.vector.tensor_copy(dst, src)
             elif engine == "g":
@@ -146,8 +147,8 @@ def tile_list_shard_fit_scores_kernel(tc, tab_words, tab_scales, offs, offs2, w1
                 )
 
         def h_relu(b, jh, c, on_vector):
-            dst = h_bf[b, jh][:, P * c : P * (c + 1), :]
-            src = h_acc[b, jh, c][:].rearrange("p u j -> p j u")
+            dst = h_bf[b, jh][:, P * c : P * (c + 1), :].rearrange("p (i l) u -> p i u l", l=2)
+            src = h_acc[b, jh, c][:].rearrange("p u (i l) -> p i u l", l=2)
             if on_vector:
                 nc.vector.tensor_scalar(dst, src, 0.0, None, ALU.max)
             else:

@@ -39,8 +39,6 @@ def tile_list_shard_fit_scores_kernel(tc, tab_words, tab_scales, offs, offs2, w1
 
         idx = keep.tile([P, S // 16], U16, name="idx")
         idx2 = keep.tile([P, S2 // 16], U16, name="idx2")
-        nc.sync.dma_start(idx2[:], offs2)
-        nc.sync.dma_start(idx[:], offs)
 
         tab_sc = held([P, T], U8, "tab_sc")
         nc.gpsimd.memset(tab_sc[:, : 5 * T // 8].bitcast(I32), 0)
@@ -55,28 +53,26 @@ def tile_list_shard_fit_scores_kernel(tc, tab_words, tab_scales, offs, offs2, w1
         w4_w = held([P, PASSES, 2 * S], U8, "w4_w")
         gain_sb = held([P, MT], F32, "gain_sb")
 
-        def load_tab(a):
-            nc.sync.dma_start(tab_w[a][:], tab_words[a].rearrange("p t i -> p (t i)").bitcast(I32))
+        def load_tab(a, c0=0, c1=T):
+            nc.sync.dma_start(tab_w[a][:, c0:c1], tab_words[a].rearrange("p t i -> p (t i)").bitcast(I32)[:, c0:c1])
 
         def load_w1(b, a, m0, m1, tag=None):
             raw = keep.tile([P, PACK, PACK * (m1 - m0)], F32, name="w1_raw%d%d_%d" % (b, a, m0), tag=tag or "w1_raw%d%d_%d" % (b, a, m0), align_bytes=64)
-            w1_raw[b, a, m0] = raw
+            w1_raw[b, a, m0] = raw[:]
             nc.sync.dma_start(
                 raw[:],
                 w1[KP * a : KP * (a + 1), KP * b + PACK * m0 : KP * b + PACK * m1].rearrange("(p t) c -> p t c", t=PACK),
             )
 
-        for q in (0, 2, 1, 3):
-            nc.sync.dma_start(tab_sc[32 * q : 32 * q + 8, :].bitcast(I32), tab_scales[:, 4 * q : 4 * q + 4, :].bitcast(I32))
-        warm = keep.tile([P, 2], F32, name="warm")
-        nc.gpsimd.memset(warm[:, 0:1], 0.0)
-        nc.scalar.activation(warm[:, 1:2], warm[:, 0:1], ACT.Relu)
-        load_tab(0)
-        load_w1(0, 0, 0, P)
-        load_w1(0, 1, 0, P)
-        load_tab(1)
-        load_w1(1, 0, 0, P)
-        load_w1(1, 1, 0, P)
+        def load_w1_rows(a):
+            raw = keep.tile([P, PACK, K], F32, name="w1_rows%d" % a, align_bytes=64)
+            for b in range(PASSES):
+                w1_raw[b, a, 0] = raw[:, :, KP * b : KP * (b + 1)]
+            nc.sync.dma_start(
+                raw[:].rearrange("p t c -> p (t c)"),
+                w1[KP * a : KP * (a + 1), :].rearrange("(p t) c -> p (t c)", t=PACK),
+            )
+
 
         v2_w = {}
         v_sc, v_w = {}, {}
@@ -106,7 +102,7 @@ def tile_list_shard_fit_scores_kernel(tc, tab_words, tab_scales, offs, offs2, w1
         def cast_w1(b, a, m0, m1, engine):
             u0, u1 = m0 // 32, m1 // 32
             dst = w1_bf[b, a][:, u0:u1, :, :].rearrange("p u m t -> p m t u")
-            src = w1_raw[b, a, 0][:].rearrange("p t (m u) -> p m t u", u=PACK)[:, :, :, u0:u1]
+            src = w1_raw[b, a, 0].rearrange("p t (m u) -> p m t u", u=PACK)[:, :, :, u0:u1]
             if engine == "v":
                 nc.vector.tensor_copy(dst, src)
             elif engine == "g":
@@ -163,10 +159,10 @@ def tile_list_shard_fit_scores_kernel(tc, tab_words, tab_scales, offs, offs2, w1
                 in_=h_bf[b, jh][:, j0:j1, :].rearrange("p j u -> p (j u)"),
             )
 
-        f_sb = {}
+        f_sb, f_acc = {}, {}
 
         def f_tile(jh, mt, on_vector):
-            if mt == 0:
+            if jh not in f_sb:
                 f_sb[jh] = keep.tile([P, MT, HALF], F32, name="f_sb%d" % jh, tag="then_f%d" % jh, align_bytes=64)
             acc = psum.tile([P, HALF], F32, name="f_acc", tag=FTAG, bufs=BUFS[FTAG])
             rows = slice(P * mt, P * (mt + 1))
@@ -180,9 +176,10 @@ def tile_list_shard_fit_scores_kernel(tc, tab_words, tab_scales, offs, offs2, w1
                     start=(a == 0),
                     stop=(a == PASSES - 1),
                 )
-            if on_vector:
+            f_acc[jh, mt] = acc
+            if on_vector == "v":
                 nc.vector.tensor_copy(f_sb[jh][:, mt, :], acc[:])
-            else:
+            elif on_vector != "k":
                 nc.scalar.activation(f_sb[jh][:, mt, :], acc[:], ACT.Copy)
 
         def e_tile(jh, mt, shared):
@@ -199,15 +196,44 @@ def tile_list_shard_fit_scores_kernel(tc, tab_words, tab_scales, offs, offs2, w1
                     stop=(b == PASSES - 1),
                 )
             best = ring.tile([P, HALF], F32, name="best")
-            nc.vector.tensor_tensor(best[:], acc[:], f_sb[jh][:, mt, :], ALU.max)
             res = ring.tile([P, HALF], F32, name="res")
-            if shared:
+            if shared == "x":
+                nc.scalar.activation(f_sb[jh][:, mt, :], acc[:], ACT.Copy)
+                nc.vector.tensor_tensor(best[:], f_acc[jh, mt][:], f_sb[jh][:, mt, :], ALU.max)
+                again = ring.tile([P, HALF], F32, name="again")
+                nc.gpsimd.tensor_scalar(again[:], f_sb[jh][:, mt, :], gain_sb[:, mt : mt + 1], 0.0, ALU.mult, ALU.add)
+                nc.gpsimd.tensor_tensor(res[:], best[:], again[:], ALU.add)
+                nc.sync.dma_start(out[rows, HALF * jh : HALF * (jh + 1)], res[:])
+                return
+            nc.vector.tensor_tensor(best[:], acc[:], f_sb[jh][:, mt, :], ALU.max)
+            if shared == "g":
                 again = ring.tile([P, HALF], F32, name="again")
                 nc.scalar.activation(again[:], acc[:], ACT.Copy, scale=gain_sb[:, mt : mt + 1])
                 nc.gpsimd.tensor_tensor(res[:], best[:], again[:], ALU.add)
             else:
                 nc.vector.scalar_tensor_tensor(res[:], acc[:], gain_sb[:, mt : mt + 1], best[:], ALU.mult, ALU.add)
             nc.sync.dma_start(out[rows, HALF * jh : HALF * (jh + 1)], res[:])
+
+        def e_half(jh, mt, jq):
+            cols = slice(jq * (HALF // 2), (jq + 1) * (HALF // 2))
+            rows = slice(P * mt, P * (mt + 1))
+            acc = psum.tile([P, HALF // 2], F32, name="eh_acc", tag=ETAG, bufs=BUFS[ETAG])
+            for b in range(PASSES):
+                nc.tensor.matmul_mx(
+                    out=acc[:],
+                    lhsT=v2_w[b][:, rows].bitcast(FP8X4),
+                    lhsT_scale=(v2_sc, v2_sc1)[b][:, rows],
+                    rhs=h_w[b, jh][:, cols].bitcast(FP8X4),
+                    rhs_scale=h_sc[b, jh][:, cols],
+                    start=(b == 0),
+                    stop=(b == PASSES - 1),
+                )
+            best = ring.tile([P, HALF // 2], F32, name="best")
+            res = ring.tile([P, HALF // 2], F32, name="res")
+            nc.vector.tensor_tensor(best[:], acc[:], f_sb[jh][:, mt, cols], ALU.max)
+            nc.vector.scalar_tensor_tensor(res[:], acc[:], gain_sb[:, mt : mt + 1], best[:], ALU.mult, ALU.add)
+            j0 = HALF * jh + cols.start
+            nc.sync.dma_start(out[rows, j0 : j0 + HALF // 2], res[:])
 
         def e_pair(jh, jq, mp, shared):
             acc = psum.tile([P, 2, HALF // 2], F32, name="e2_acc", tag=ETAG, bufs=BUFS[ETAG])
@@ -240,24 +266,42 @@ def tile_list_shard_fit_scores_kernel(tc, tab_words, tab_scales, offs, offs2, w1
             j0 = HALF * jh + cols.start
             nc.sync.dma_start(out[2 * P * mp : 2 * P * (mp + 1), j0 : j0 + HALF // 2].rearrange("(i p) j -> p i j", p=P), res[:])
 
+        load_tab(0, 0, T // 2)
+        load_tab(0, T // 2, T)
+        nc.sync.dma_start(idx[:], offs)
+        nc.sync.dma_start(idx2[:], offs2)
+        for q in (0, 2, 1, 3):
+            nc.sync.dma_start(tab_sc[32 * q : 32 * q + 8, :].bitcast(I32), tab_scales[:, 4 * q : 4 * q + 4, :].bitcast(I32))
+        warm = keep.tile([P, 2], F32, name="warm")
+        nc.gpsimd.memset(warm[:, 0:1], 0.0)
+        nc.scalar.activation(warm[:, 1:2], warm[:, 0:1], ACT.Relu)
+        load_w1(0, 0, 0, P)
+        load_w1(0, 1, 0, P)
+        load_w1(1, 0, 0, P)
+        load_tab(1)
         gather_v(0, 0, "v_w00")
-        gather_v(0, 1, "v_w01")
-        gather_v2(0, "v2_w0")
         gather_v_sc(0, "v_sc0")
+        gather_v(0, 1, "v_w01")
+        gather_v_sc(1, "v_sc1")
         v2_sc = keep.tile([P, S2], U8, name="v2_sc", tag="v2_sc", align_bytes=64)
         nc.vector.tensor_copy(v2_sc[:], tab_sc[:].indirect(idx2[:]))
         nc.sync.dma_start(v2_sc1[0 : P - 4, :].bitcast(I32), v2_sc[4:P, :].bitcast(I32))
+        gather_v2(0, "v2_w0")
         for q in (0, 2, 1, 3):
             nc.sync.dma_start(w4_sc[32 * q : 32 * q + 4, :, :].bitcast(I32), w4_scales[:, 4 * q : 4 * q + 4, :].rearrange("a r n -> r a n").bitcast(I32))
+        load_w1(1, 1, 0, P)
         nc.sync.dma_start(w4_w[:].bitcast(I32), w4_words.rearrange("a p n -> p a n").bitcast(I32))
         with nc.allow_non_contiguous_dma(reason="one gain for each partition and row tile"):
             nc.sync.dma_start(gain_sb[:], gain.rearrange("(c p) -> p c", p=P))
         cast_w1(0, 0, 0, P // 2, "s")
         cast_w1(0, 0, P // 2, P, "s")
-        quant_w1(0, 0)
-        gather_v_sc(1, "w1_bf00")
         cast_w1(0, 1, 0, P // 2, "s")
         cast_w1(0, 1, P // 2, P, "s")
+        quant_w1(0, 0)
+        cast_w1(1, 0, 0, P // 2, "v")
+        cast_w1(1, 0, P // 2, P, "s")
+        quant_w1(0, 1)
+        quant_w1(1, 0)
         h_pass(0, 0, 0, 0)
         h_pass(0, 0, 1, 0)
         h_pass(0, 0, 2, 0)
@@ -267,10 +311,8 @@ def tile_list_shard_fit_scores_kernel(tc, tab_words, tab_scales, offs, offs2, w1
         h_pass(0, 1, 2, 0)
         h_pass(0, 1, 3, 0)
         gather_v(1, 0, "v_w10")
-        quant_w1(0, 1)
-        gather_v(1, 1, "w1_bf01")
-        cast_w1(1, 0, 0, P // 2, "v")
-        cast_w1(1, 0, P // 2, P, "s")
+        gather_v(1, 1, "v_w11")
+        gather_v2(1, "v2_w1")
         h_pass(0, 0, 0, 1)
         h_relu(0, 0, 0, False)
         h_pass(0, 0, 1, 1)
@@ -287,19 +329,12 @@ def tile_list_shard_fit_scores_kernel(tc, tab_words, tab_scales, offs, offs2, w1
         h_relu(0, 1, 2, False)
         h_pass(0, 1, 3, 1)
         h_relu(0, 1, 3, False)
-        quant_w1(1, 0)
-        cast_w1(1, 1, 0, P // 2, "v")
-        cast_w1(1, 1, P // 2, P, "v")
+        cast_w1(1, 1, 0, P, "v")
         h_pass(1, 0, 0, 0)
         h_pass(1, 0, 1, 0)
         h_pass(1, 0, 2, 0)
         h_pass(1, 0, 3, 0)
-        h_pass(1, 1, 0, 0)
-        h_pass(1, 1, 1, 0)
-        h_pass(1, 1, 2, 0)
-        h_pass(1, 1, 3, 0)
         quant_w1(1, 1)
-        gather_v2(1, "w1_bf11")
         quant_h(0, 0, "h_w00")
         quant_h(0, 1, "h_bf00")
         h_pass(1, 0, 0, 1)
@@ -311,28 +346,32 @@ def tile_list_shard_fit_scores_kernel(tc, tab_words, tab_scales, offs, offs2, w1
         h_pass(1, 0, 3, 1)
         h_relu(1, 0, 3, False)
         quant_h(1, 0, "h_w10")
-        f_tile(0, 0, False)
-        f_tile(0, 1, False)
-        e_tile(0, 0, False)
+        f_tile(0, 0, ".")
+        f_tile(0, 1, ".")
+        e_tile(0, 0, "g")
+        h_pass(1, 1, 0, 0)
         h_pass(1, 1, 0, 1)
         h_relu(1, 1, 0, False)
-        e_tile(0, 1, False)
+        e_tile(0, 1, ".")
+        h_pass(1, 1, 1, 0)
         h_pass(1, 1, 1, 1)
         h_relu(1, 1, 1, False)
+        h_pass(1, 1, 2, 0)
         h_pass(1, 1, 2, 1)
         h_relu(1, 1, 2, False)
+        h_pass(1, 1, 3, 0)
         h_pass(1, 1, 3, 1)
         h_relu(1, 1, 3, False)
         quant_h(1, 1, "h_w11")
-        f_tile(0, 2, False)
-        e_tile(0, 2, False)
-        f_tile(0, 3, False)
-        e_tile(0, 3, False)
-        f_tile(1, 0, False)
-        e_tile(1, 0, False)
-        f_tile(1, 1, False)
-        e_tile(1, 1, False)
-        f_tile(1, 2, False)
-        e_tile(1, 2, False)
-        f_tile(1, 3, False)
-        e_tile(1, 3, False)
+        f_tile(0, 2, ".")
+        e_tile(0, 2, "g")
+        f_tile(0, 3, ".")
+        e_tile(0, 3, ".")
+        f_tile(1, 0, ".")
+        e_tile(1, 0, "g")
+        f_tile(1, 1, ".")
+        e_tile(1, 1, ".")
+        f_tile(1, 2, ".")
+        e_tile(1, 2, ".")
+        f_tile(1, 3, ".")
+        e_tile(1, 3, ".")

@@ -21,128 +21,113 @@ PACK = 4
 KP = P * PACK
 PASSES = K // KP
 HALF = 512
-NH = S // HALF
-MT = S2 // P
-FTAG, ETAG, HTAG = "acc", "acc", "acc"
-BUFS = {"acc": 8}
+CHUNKS = HALF // P
+ROW_TILES = S2 // P
+PSUM_BANKS = 8
+EPILOGUE_BUFS = 4
+LIST_ROWS = 16
+PLANE_ROWS = 4
+QUADRANT_ORDER = (0, 2, 1, 3)
+GPSIMD_ZERO_COLS = 5 * T // 8
 
 
-def tile_list_shard_fit_scores_kernel(tc, tab_words, tab_scales, offs, offs2, w1, w4_words, w4_scales, gain, out):
+def tile_list_shard_fit_scores_kernel(
+    tc, tab_words, tab_scales, offs, offs2, w1, w4_words, w4_scales, gain, out
+):
     nc = tc.nc
     with ExitStack() as ctx:
         keep = ctx.enter_context(tc.tile_pool(name="keep", bufs=1))
-        ring = ctx.enter_context(tc.tile_pool(name="ring", bufs=4))
-        psum = ctx.enter_context(tc.psum_pool(name="psum", bufs=4))
+        ring = ctx.enter_context(tc.tile_pool(name="ring", bufs=EPILOGUE_BUFS))
+        psum = ctx.enter_context(tc.psum_pool(name="psum", bufs=PSUM_BANKS))
 
-        def held(shape, dtype, name):
-            return keep.tile(shape, dtype, name=name, align_bytes=64)
+        def held(shape, dtype, name, reuses=None):
+            return keep.tile(shape, dtype, name=name, tag=reuses or name, align_bytes=64)
 
-        idx = keep.tile([P, S // 16], U16, name="idx")
-        idx2 = keep.tile([P, S2 // 16], U16, name="idx2")
+        idx = keep.tile([P, S // LIST_ROWS], U16, name="idx")
+        idx2 = keep.tile([P, S2 // LIST_ROWS], U16, name="idx2")
 
         tab_sc = held([P, T], U8, "tab_sc")
-        nc.gpsimd.memset(tab_sc[:, : 5 * T // 8].bitcast(I32), 0)
-        nc.vector.memset(tab_sc[:, 5 * T // 8 :].bitcast(I32), 0)
+        nc.gpsimd.memset(tab_sc[:, :GPSIMD_ZERO_COLS].bitcast(I32), 0)
+        nc.vector.memset(tab_sc[:, GPSIMD_ZERO_COLS:].bitcast(I32), 0)
         w4_sc = held([P, PASSES, S], U8, "w4_sc")
         nc.vector.memset(w4_sc[:].rearrange("p a n -> p (a n)").bitcast(I32), 0)
         v2_sc1 = held([P, S2], U8, "v2_sc1")
         nc.vector.memset(v2_sc1[:].bitcast(I32), 0)
 
         tab_w = [held([P, T], I32, "tab_w%d" % a) for a in range(PASSES)]
-        w1_raw = {}
         w4_w = held([P, PASSES, 2 * S], U8, "w4_w")
-        gain_sb = held([P, MT], F32, "gain_sb")
-
-        def load_tab(a, c0=0, c1=T):
-            nc.sync.dma_start(tab_w[a][:, c0:c1], tab_words[a].rearrange("p t i -> p (t i)").bitcast(I32)[:, c0:c1])
-
-        def load_w1(b, a, m0, m1, tag=None):
-            raw = keep.tile([P, PACK, PACK * (m1 - m0)], F32, name="w1_raw%d%d_%d" % (b, a, m0), tag=tag or "w1_raw%d%d_%d" % (b, a, m0), align_bytes=64)
-            w1_raw[b, a, m0] = raw[:]
-            nc.sync.dma_start(
-                raw[:],
-                w1[KP * a : KP * (a + 1), KP * b + PACK * m0 : KP * b + PACK * m1].rearrange("(p t) c -> p t c", t=PACK),
-            )
-
-        def load_w1_rows(a):
-            raw = keep.tile([P, PACK, K], F32, name="w1_rows%d" % a, align_bytes=64)
-            for b in range(PASSES):
-                w1_raw[b, a, 0] = raw[:, :, KP * b : KP * (b + 1)]
-            nc.sync.dma_start(
-                raw[:].rearrange("p t c -> p (t c)"),
-                w1[KP * a : KP * (a + 1), :].rearrange("(p t) c -> p (t c)", t=PACK),
-            )
-
-
-        v2_w = {}
-        v_sc, v_w = {}, {}
-
-        def half(jh):
-            return idx[:, jh * (HALF // 16) : (jh + 1) * (HALF // 16)]
-
-        def gather_v_sc(jh, tag):
-            v_sc[jh] = keep.tile([P, HALF], U8, name="v_sc%d" % jh, tag=tag, align_bytes=64)
-            nc.vector.tensor_copy(v_sc[jh][:], tab_sc[:].indirect(half(jh)))
-
-        def gather_v(a, jh, tag):
-            v_w[a, jh] = keep.tile([P, HALF], U32, name="v_w%d%d" % (a, jh), tag=tag, align_bytes=64)
-            nc.vector.tensor_copy(v_w[a, jh][:], tab_w[a][:].bitcast(U32).indirect(half(jh)))
-
-        def gather_v2(a, tag):
-            v2_w[a] = keep.tile([P, S2], U32, name="v2_w%d" % a, tag=tag, align_bytes=64)
-            nc.vector.tensor_copy(v2_w[a][:], tab_w[a][:].bitcast(U32).indirect(idx2[:]))
-
-        w1_bf, w1_w, w1_sc = {}, {}, {}
+        gain_sb = held([P, ROW_TILES], F32, "gain_sb")
+        w1_raw, w1_bf, w1_w, w1_sc = {}, {}, {}, {}
+        h_bf, h_w, h_sc, h_acc = {}, {}, {}, {}
+        v_w, v_sc, v2_w, f_sb = {}, {}, {}, {}
         for b in range(PASSES):
             for a in range(PASSES):
                 w1_bf[b, a] = held([P, PACK, P, PACK], BF16, "w1_bf%d%d" % (b, a))
                 w1_w[b, a] = held([P, KP], U32, "w1_w%d%d" % (b, a))
                 w1_sc[b, a] = held([P, KP], U8, "w1_sc%d%d" % (b, a))
+            for jh in range(S // HALF):
+                h_bf[b, jh] = held([P, HALF, PACK], BF16, "h_bf%d%d" % (b, jh))
+                h_sc[b, jh] = held([P, HALF], U8, "h_sc%d%d" % (b, jh))
+        for jh in range(S // HALF):
+            f_sb[jh] = held([P, ROW_TILES, HALF], F32, "f_sb%d" % jh)
 
-        def cast_w1(b, a, m0, m1, engine):
-            u0, u1 = m0 // 32, m1 // 32
+        def load_tab(a, t0, t1):
+            words = tab_words[a].rearrange("p t i -> p (t i)").bitcast(I32)
+            nc.sync.dma_start(tab_w[a][:, t0:t1], words[:, t0:t1])
+
+        def load_w1(b, a):
+            w1_raw[b, a] = held([P, PACK, KP], F32, "w1_raw%d%d" % (b, a))
+            block = w1[KP * a : KP * (a + 1), KP * b : KP * (b + 1)]
+            nc.sync.dma_start(w1_raw[b, a][:], block.rearrange("(p t) c -> p t c", t=PACK))
+
+        def entries(jh):
+            return idx[:, jh * (HALF // LIST_ROWS) : (jh + 1) * (HALF // LIST_ROWS)]
+
+        def gather_v(a, jh, reuses=None):
+            v_w[a, jh] = held([P, HALF], U32, "v_w%d%d" % (a, jh), reuses)
+            nc.vector.tensor_copy(v_w[a, jh][:], tab_w[a][:].bitcast(U32).indirect(entries(jh)))
+
+        def gather_v_scales(jh):
+            v_sc[jh] = held([P, HALF], U8, "v_sc%d" % jh)
+            nc.vector.tensor_copy(v_sc[jh][:], tab_sc[:].indirect(entries(jh)))
+
+        def gather_v2(a):
+            v2_w[a] = held([P, S2], U32, "v2_w%d" % a)
+            nc.vector.tensor_copy(v2_w[a][:], tab_w[a][:].bitcast(U32).indirect(idx2[:]))
+
+        def cast_w1(b, a, u0, u1, on_vector):
             dst = w1_bf[b, a][:, u0:u1, :, :].rearrange("p u m t -> p m t u")
-            src = w1_raw[b, a, 0].rearrange("p t (m u) -> p m t u", u=PACK)[:, :, :, u0:u1]
-            if engine == "v":
+            src = w1_raw[b, a][:].rearrange("p t (m u) -> p m t u", u=PACK)[:, :, :, u0:u1]
+            if on_vector:
                 nc.vector.tensor_copy(dst, src)
-            elif engine == "g":
-                nc.gpsimd.tensor_scalar(dst, src, 1.0, 0.0, ALU.mult, ALU.add)
             else:
                 nc.scalar.activation(dst, src, ACT.Copy)
 
-        def quant_w1(b, a):
+        def quantize_w1(b, a):
             nc.vector.quantize_mx(
                 out=w1_w[b, a][:].bitcast(FP8X4),
                 scales=w1_sc[b, a][:],
                 in_=w1_bf[b, a][:].rearrange("p u m t -> p (u m t)"),
             )
 
-        h_bf, h_w, h_sc = {}, {}, {}
-        for b in range(PASSES):
-            for jh in range(NH):
-                h_bf[b, jh] = held([P, HALF, PACK], BF16, "h_bf%d%d" % (b, jh))
-                h_sc[b, jh] = held([P, HALF], U8, "h_sc%d%d" % (b, jh))
-
-        h_acc = {}
-
         def h_pass(b, jh, c, a):
             if a == 0:
-                h_acc[b, jh, c] = psum.tile([P, PACK, P], F32, name="h_acc", tag=HTAG, bufs=BUFS[HTAG])
-            acc = h_acc[b, jh, c]
+                h_acc[b, jh, c] = psum.tile([P, PACK, P], F32, name="h_acc", tag="bank")
             cols = slice(P * c, P * (c + 1))
             for u in range(PACK):
                 rows = slice(P * u, P * (u + 1))
                 nc.tensor.matmul_mx(
-                    out=acc[:, u, :],
+                    out=h_acc[b, jh, c][:, u, :],
                     lhsT=w1_w[b, a][:, rows].bitcast(FP8X4),
                     lhsT_scale=w1_sc[b, a][:, rows],
                     rhs=v_w[a, jh][:, cols].bitcast(FP8X4),
-                    rhs_scale=v_sc[jh][4 * a :, cols],
+                    rhs_scale=v_sc[jh][PLANE_ROWS * a :, cols],
                     start=(a == 0 and u == 0),
                     stop=(a == PASSES - 1 and u == PACK - 1),
                 )
 
-        def h_relu(b, jh, c, on_vector):
+        def h_finish(b, jh, c, on_vector=False):
+            h_pass(b, jh, c, PASSES - 1)
             dst = h_bf[b, jh][:, P * c : P * (c + 1), :].rearrange("p (i l) u -> p i u l", l=2)
             src = h_acc[b, jh, c][:].rearrange("p u (i l) -> p i u l", l=2)
             if on_vector:
@@ -150,228 +135,118 @@ def tile_list_shard_fit_scores_kernel(tc, tab_words, tab_scales, offs, offs2, w1
             else:
                 nc.scalar.activation(dst, src, ACT.Relu)
 
-        def quant_h(b, jh, tag, j0=0, j1=HALF):
-            if j0 == 0:
-                h_w[b, jh] = keep.tile([P, HALF], U32, name="h_w%d%d" % (b, jh), tag=tag, align_bytes=64)
+        def quantize_h(b, jh, reuses=None):
+            h_w[b, jh] = held([P, HALF], U32, "h_w%d%d" % (b, jh), reuses)
             nc.vector.quantize_mx(
-                out=h_w[b, jh][:, j0:j1].bitcast(FP8X4),
-                scales=h_sc[b, jh][:, j0:j1],
-                in_=h_bf[b, jh][:, j0:j1, :].rearrange("p j u -> p (j u)"),
+                out=h_w[b, jh][:].bitcast(FP8X4),
+                scales=h_sc[b, jh][:],
+                in_=h_bf[b, jh][:].rearrange("p j u -> p (j u)"),
             )
 
-        f_sb, f_acc = {}, {}
-
-        def f_tile(jh, mt, on_vector):
-            if jh not in f_sb:
-                f_sb[jh] = keep.tile([P, MT, HALF], F32, name="f_sb%d" % jh, tag="then_f%d" % jh, align_bytes=64)
-            acc = psum.tile([P, HALF], F32, name="f_acc", tag=FTAG, bufs=BUFS[FTAG])
+        def v2_product(acc, mt, moving, moving_scales):
             rows = slice(P * mt, P * (mt + 1))
             for a in range(PASSES):
                 nc.tensor.matmul_mx(
                     out=acc[:],
                     lhsT=v2_w[a][:, rows].bitcast(FP8X4),
-                    lhsT_scale=(v2_sc, v2_sc1)[a][:, rows],
-                    rhs=w4_w[:, a, 2 * HALF * jh : 2 * HALF * (jh + 1)].bitcast(FP4X4),
-                    rhs_scale=w4_sc[:, a, HALF * jh : HALF * (jh + 1)],
+                    lhsT_scale=v2_planes[a][:, rows],
+                    rhs=moving(a),
+                    rhs_scale=moving_scales(a),
                     start=(a == 0),
                     stop=(a == PASSES - 1),
                 )
-            f_acc[jh, mt] = acc
-            if on_vector == "v":
-                nc.vector.tensor_copy(f_sb[jh][:, mt, :], acc[:])
-            elif on_vector != "k":
-                nc.scalar.activation(f_sb[jh][:, mt, :], acc[:], ACT.Copy)
 
-        def e_tile(jh, mt, shared):
-            acc = psum.tile([P, HALF], F32, name="e_acc", tag=ETAG, bufs=BUFS[ETAG])
-            rows = slice(P * mt, P * (mt + 1))
-            for b in range(PASSES):
-                nc.tensor.matmul_mx(
-                    out=acc[:],
-                    lhsT=v2_w[b][:, rows].bitcast(FP8X4),
-                    lhsT_scale=(v2_sc, v2_sc1)[b][:, rows],
-                    rhs=h_w[b, jh][:].bitcast(FP8X4),
-                    rhs_scale=h_sc[b, jh][:],
-                    start=(b == 0),
-                    stop=(b == PASSES - 1),
-                )
+        def f_tile(jh, mt):
+            acc = psum.tile([P, HALF], F32, name="f_acc", tag="bank")
+            v2_product(
+                acc,
+                mt,
+                lambda a: w4_w[:, a, 2 * HALF * jh : 2 * HALF * (jh + 1)].bitcast(FP4X4),
+                lambda a: w4_sc[:, a, HALF * jh : HALF * (jh + 1)],
+            )
+            nc.scalar.activation(f_sb[jh][:, mt, :], acc[:], ACT.Copy)
+
+        def e_tile(jh, mt):
+            acc = psum.tile([P, HALF], F32, name="e_acc", tag="bank")
+            v2_product(acc, mt, lambda b: h_w[b, jh][:].bitcast(FP8X4), lambda b: h_sc[b, jh][:])
             best = ring.tile([P, HALF], F32, name="best")
             res = ring.tile([P, HALF], F32, name="res")
-            if shared == "x":
-                nc.scalar.activation(f_sb[jh][:, mt, :], acc[:], ACT.Copy)
-                nc.vector.tensor_tensor(best[:], f_acc[jh, mt][:], f_sb[jh][:, mt, :], ALU.max)
-                again = ring.tile([P, HALF], F32, name="again")
-                nc.gpsimd.tensor_scalar(again[:], f_sb[jh][:, mt, :], gain_sb[:, mt : mt + 1], 0.0, ALU.mult, ALU.add)
-                nc.gpsimd.tensor_tensor(res[:], best[:], again[:], ALU.add)
-                nc.sync.dma_start(out[rows, HALF * jh : HALF * (jh + 1)], res[:])
-                return
             nc.vector.tensor_tensor(best[:], acc[:], f_sb[jh][:, mt, :], ALU.max)
-            if shared == "g":
-                again = ring.tile([P, HALF], F32, name="again")
-                nc.scalar.activation(again[:], acc[:], ACT.Copy, scale=gain_sb[:, mt : mt + 1])
-                nc.gpsimd.tensor_tensor(res[:], best[:], again[:], ALU.add)
-            else:
-                nc.vector.scalar_tensor_tensor(res[:], acc[:], gain_sb[:, mt : mt + 1], best[:], ALU.mult, ALU.add)
-            nc.sync.dma_start(out[rows, HALF * jh : HALF * (jh + 1)], res[:])
-
-        def e_half(jh, mt, jq):
-            cols = slice(jq * (HALF // 2), (jq + 1) * (HALF // 2))
-            rows = slice(P * mt, P * (mt + 1))
-            acc = psum.tile([P, HALF // 2], F32, name="eh_acc", tag=ETAG, bufs=BUFS[ETAG])
-            for b in range(PASSES):
-                nc.tensor.matmul_mx(
-                    out=acc[:],
-                    lhsT=v2_w[b][:, rows].bitcast(FP8X4),
-                    lhsT_scale=(v2_sc, v2_sc1)[b][:, rows],
-                    rhs=h_w[b, jh][:, cols].bitcast(FP8X4),
-                    rhs_scale=h_sc[b, jh][:, cols],
-                    start=(b == 0),
-                    stop=(b == PASSES - 1),
-                )
-            best = ring.tile([P, HALF // 2], F32, name="best")
-            res = ring.tile([P, HALF // 2], F32, name="res")
-            nc.vector.tensor_tensor(best[:], acc[:], f_sb[jh][:, mt, cols], ALU.max)
             nc.vector.scalar_tensor_tensor(res[:], acc[:], gain_sb[:, mt : mt + 1], best[:], ALU.mult, ALU.add)
-            j0 = HALF * jh + cols.start
-            nc.sync.dma_start(out[rows, j0 : j0 + HALF // 2], res[:])
-
-        def e_pair(jh, jq, mp, shared):
-            acc = psum.tile([P, 2, HALF // 2], F32, name="e2_acc", tag=ETAG, bufs=BUFS[ETAG])
-            cols = slice(jq * (HALF // 2), (jq + 1) * (HALF // 2))
-            for i in range(2):
-                rows = slice(P * (2 * mp + i), P * (2 * mp + i + 1))
-                for b in range(PASSES):
-                    nc.tensor.matmul_mx(
-                        out=acc[:, i, :],
-                        lhsT=v2_w[b][:, rows].bitcast(FP8X4),
-                        lhsT_scale=(v2_sc, v2_sc1)[b][:, rows],
-                        rhs=h_w[b, jh][:, cols].bitcast(FP8X4),
-                        rhs_scale=h_sc[b, jh][:, cols],
-                        start=(b == 0),
-                        stop=(b == PASSES - 1),
-                    )
-            best = ring.tile([P, 2, HALF // 2], F32, name="best")
-            nc.vector.tensor_tensor(best[:], acc[:], f_sb[jh][:, 2 * mp : 2 * mp + 2, cols], ALU.max)
-            res = ring.tile([P, 2, HALF // 2], F32, name="res")
-            if shared:
-                again = ring.tile([P, 2, HALF // 2], F32, name="again")
-                for i in range(2):
-                    mt = 2 * mp + i
-                    nc.scalar.activation(again[:, i, :], acc[:, i, :], ACT.Copy, scale=gain_sb[:, mt : mt + 1])
-                nc.gpsimd.tensor_tensor(res[:], best[:], again[:], ALU.add)
-            else:
-                for i in range(2):
-                    mt = 2 * mp + i
-                    nc.vector.scalar_tensor_tensor(res[:, i, :], acc[:, i, :], gain_sb[:, mt : mt + 1], best[:, i, :], ALU.mult, ALU.add)
-            j0 = HALF * jh + cols.start
-            nc.sync.dma_start(out[2 * P * mp : 2 * P * (mp + 1), j0 : j0 + HALF // 2].rearrange("(i p) j -> p i j", p=P), res[:])
+            nc.sync.dma_start(out[P * mt : P * (mt + 1), HALF * jh : HALF * (jh + 1)], res[:])
 
         load_tab(0, 0, T // 2)
         load_tab(0, T // 2, T)
         nc.sync.dma_start(idx[:], offs)
         nc.sync.dma_start(idx2[:], offs2)
-        for q in (0, 2, 1, 3):
-            nc.sync.dma_start(tab_sc[32 * q : 32 * q + 8, :].bitcast(I32), tab_scales[:, 4 * q : 4 * q + 4, :].bitcast(I32))
-        warm = keep.tile([P, 2], F32, name="warm")
-        nc.gpsimd.memset(warm[:, 0:1], 0.0)
-        nc.scalar.activation(warm[:, 1:2], warm[:, 0:1], ACT.Relu)
-        load_w1(0, 0, 0, P)
-        load_w1(0, 1, 0, P)
-        load_w1(1, 0, 0, P)
-        load_tab(1)
-        gather_v(0, 0, "v_w00")
-        gather_v_sc(0, "v_sc0")
-        gather_v(0, 1, "v_w01")
-        gather_v_sc(1, "v_sc1")
-        v2_sc = keep.tile([P, S2], U8, name="v2_sc", tag="v2_sc", align_bytes=64)
+        for q in QUADRANT_ORDER:
+            nc.sync.dma_start(
+                tab_sc[32 * q : 32 * q + PASSES * PLANE_ROWS, :].bitcast(I32),
+                tab_scales[:, PLANE_ROWS * q : PLANE_ROWS * (q + 1), :].bitcast(I32),
+            )
+        load_w1(0, 0)
+        load_w1(0, 1)
+        load_w1(1, 0)
+        load_tab(1, 0, T)
+
+        for jh in range(S // HALF):
+            gather_v(0, jh)
+            gather_v_scales(jh)
+        v2_sc = held([P, S2], U8, "v2_sc")
         nc.vector.tensor_copy(v2_sc[:], tab_sc[:].indirect(idx2[:]))
-        nc.sync.dma_start(v2_sc1[0 : P - 4, :].bitcast(I32), v2_sc[4:P, :].bitcast(I32))
-        gather_v2(0, "v2_w0")
-        for q in (0, 2, 1, 3):
-            nc.sync.dma_start(w4_sc[32 * q : 32 * q + 4, :, :].bitcast(I32), w4_scales[:, 4 * q : 4 * q + 4, :].rearrange("a r n -> r a n").bitcast(I32))
-        load_w1(1, 1, 0, P)
+        nc.sync.dma_start(v2_sc1[0 : P - PLANE_ROWS, :].bitcast(I32), v2_sc[PLANE_ROWS:P, :].bitcast(I32))
+        v2_planes = (v2_sc, v2_sc1)
+        gather_v2(0)
+
+        for q in QUADRANT_ORDER:
+            nc.sync.dma_start(
+                w4_sc[32 * q : 32 * q + PLANE_ROWS, :, :].bitcast(I32),
+                w4_scales[:, PLANE_ROWS * q : PLANE_ROWS * (q + 1), :].rearrange("a r n -> r a n").bitcast(I32),
+            )
+        load_w1(1, 1)
         nc.sync.dma_start(w4_w[:].bitcast(I32), w4_words.rearrange("a p n -> p a n").bitcast(I32))
         with nc.allow_non_contiguous_dma(reason="one gain for each partition and row tile"):
             nc.sync.dma_start(gain_sb[:], gain.rearrange("(c p) -> p c", p=P))
-        cast_w1(0, 0, 0, P // 2, "s")
-        cast_w1(0, 0, P // 2, P, "s")
-        cast_w1(0, 1, 0, P // 2, "s")
-        cast_w1(0, 1, P // 2, P, "s")
-        quant_w1(0, 0)
-        cast_w1(1, 0, 0, P // 2, "v")
-        cast_w1(1, 0, P // 2, P, "s")
-        quant_w1(0, 1)
-        quant_w1(1, 0)
-        h_pass(0, 0, 0, 0)
-        h_pass(0, 0, 1, 0)
-        h_pass(0, 0, 2, 0)
-        h_pass(0, 0, 3, 0)
-        h_pass(0, 1, 0, 0)
-        h_pass(0, 1, 1, 0)
-        h_pass(0, 1, 2, 0)
-        h_pass(0, 1, 3, 0)
-        gather_v(1, 0, "v_w10")
-        gather_v(1, 1, "v_w11")
-        gather_v2(1, "v2_w1")
-        h_pass(0, 0, 0, 1)
-        h_relu(0, 0, 0, False)
-        h_pass(0, 0, 1, 1)
-        h_relu(0, 0, 1, False)
-        h_pass(0, 0, 2, 1)
-        h_relu(0, 0, 2, False)
-        h_pass(0, 0, 3, 1)
-        h_relu(0, 0, 3, False)
-        h_pass(0, 1, 0, 1)
-        h_relu(0, 1, 0, False)
-        h_pass(0, 1, 1, 1)
-        h_relu(0, 1, 1, False)
-        h_pass(0, 1, 2, 1)
-        h_relu(0, 1, 2, False)
-        h_pass(0, 1, 3, 1)
-        h_relu(0, 1, 3, False)
-        cast_w1(1, 1, 0, P, "v")
-        h_pass(1, 0, 0, 0)
-        h_pass(1, 0, 1, 0)
-        h_pass(1, 0, 2, 0)
-        h_pass(1, 0, 3, 0)
-        quant_w1(1, 1)
-        quant_h(0, 0, "h_w00")
-        quant_h(0, 1, "h_bf00")
-        h_pass(1, 0, 0, 1)
-        h_relu(1, 0, 0, False)
-        h_pass(1, 0, 1, 1)
-        h_relu(1, 0, 1, False)
-        h_pass(1, 0, 2, 1)
-        h_relu(1, 0, 2, True)
-        h_pass(1, 0, 3, 1)
-        h_relu(1, 0, 3, False)
-        quant_h(1, 0, "h_w10")
-        f_tile(0, 0, ".")
-        f_tile(0, 1, ".")
-        e_tile(0, 0, "g")
-        h_pass(1, 1, 0, 0)
-        h_pass(1, 1, 0, 1)
-        h_relu(1, 1, 0, False)
-        e_tile(0, 1, ".")
-        h_pass(1, 1, 1, 0)
-        h_pass(1, 1, 1, 1)
-        h_relu(1, 1, 1, False)
-        h_pass(1, 1, 2, 0)
-        h_pass(1, 1, 2, 1)
-        h_relu(1, 1, 2, False)
-        h_pass(1, 1, 3, 0)
-        h_pass(1, 1, 3, 1)
-        h_relu(1, 1, 3, False)
-        quant_h(1, 1, "h_w11")
-        f_tile(0, 2, ".")
-        e_tile(0, 2, "g")
-        f_tile(0, 3, ".")
-        e_tile(0, 3, ".")
-        f_tile(1, 0, ".")
-        e_tile(1, 0, "g")
-        f_tile(1, 1, ".")
-        e_tile(1, 1, ".")
-        f_tile(1, 2, ".")
-        e_tile(1, 2, ".")
-        f_tile(1, 3, ".")
-        e_tile(1, 3, ".")
+
+        for a in range(PASSES):
+            for u0 in range(0, PACK, 2):
+                cast_w1(0, a, u0, u0 + 2, on_vector=False)
+        quantize_w1(0, 0)
+        cast_w1(1, 0, 0, 2, on_vector=True)
+        cast_w1(1, 0, 2, PACK, on_vector=False)
+        quantize_w1(0, 1)
+        quantize_w1(1, 0)
+
+        for jh in range(S // HALF):
+            for c in range(CHUNKS):
+                h_pass(0, jh, c, 0)
+        gather_v(1, 0, reuses="w1_bf01")
+        gather_v(1, 1, reuses="w1_bf10")
+        gather_v2(1)
+        for jh in range(S // HALF):
+            for c in range(CHUNKS):
+                h_finish(0, jh, c)
+
+        cast_w1(1, 1, 0, PACK, on_vector=True)
+        for c in range(CHUNKS):
+            h_pass(1, 0, c, 0)
+        quantize_w1(1, 1)
+        quantize_h(0, 0, reuses="w1_bf11")
+        quantize_h(0, 1, reuses="h_bf00")
+
+        for c in range(CHUNKS):
+            h_finish(1, 0, c, on_vector=(c == CHUNKS - 2))
+        quantize_h(1, 0)
+
+        f_tile(0, 0)
+        f_tile(0, 1)
+        for c in range(CHUNKS):
+            if c < 2:
+                e_tile(0, c)
+            h_pass(1, 1, c, 0)
+            h_finish(1, 1, c)
+        quantize_h(1, 1)
+        for tile_no in range(2, (S // HALF) * ROW_TILES):
+            jh, mt = divmod(tile_no, ROW_TILES)
+            f_tile(jh, mt)
+            e_tile(jh, mt)

from contextlib import ExitStack

import concourse.mybir as mybir

K, T, S, S2 = 1024, 2048, 1024, 512
FLOPS = 2 * K * K * S + 2 * 2 * K * S2 * S

F32 = mybir.dt.float32
BF16 = mybir.dt.bfloat16
I32 = mybir.dt.int32
U32 = mybir.dt.uint32
U16 = mybir.dt.uint16
U8 = mybir.dt.uint8
FP8X4 = mybir.dt.float8_e4m3fn_x4
FP4X4 = mybir.dt.float4_e2m1fn_x4
ACT = mybir.ActivationFunctionType
ALU = mybir.AluOpType

P = 128
PACK = 4
KP = P * PACK
PASSES = K // KP
HALF = 512
CHUNKS = HALF // P
ROW_TILES = S2 // P
PSUM_BANKS = 8
EPILOGUE_BUFS = 4
LIST_ROWS = 16
PLANE_ROWS = 4
QUADRANT_ORDER = (0, 2, 1, 3)
GPSIMD_ZERO_COLS = 5 * T // 8


def tile_list_shard_fit_scores_kernel(
    tc, tab_words, tab_scales, offs, offs2, w1, w4_words, w4_scales, gain, out
):
    nc = tc.nc
    with ExitStack() as ctx:
        keep = ctx.enter_context(tc.tile_pool(name="keep", bufs=1))
        ring = ctx.enter_context(tc.tile_pool(name="ring", bufs=EPILOGUE_BUFS))
        psum = ctx.enter_context(tc.psum_pool(name="psum", bufs=PSUM_BANKS))

        def held(shape, dtype, name, reuses=None):
            return keep.tile(shape, dtype, name=name, tag=reuses or name, align_bytes=64)

        idx = keep.tile([P, S // LIST_ROWS], U16, name="idx")
        idx2 = keep.tile([P, S2 // LIST_ROWS], U16, name="idx2")

        tab_sc = held([P, T], U8, "tab_sc")
        nc.gpsimd.memset(tab_sc[:, :GPSIMD_ZERO_COLS].bitcast(I32), 0)
        nc.vector.memset(tab_sc[:, GPSIMD_ZERO_COLS:].bitcast(I32), 0)
        w4_sc = held([P, PASSES, S], U8, "w4_sc")
        nc.vector.memset(w4_sc[:].rearrange("p a n -> p (a n)").bitcast(I32), 0)
        v2_sc1 = held([P, S2], U8, "v2_sc1")
        nc.vector.memset(v2_sc1[:].bitcast(I32), 0)

        tab_w = [held([P, T], I32, "tab_w%d" % a) for a in range(PASSES)]
        w4_w = held([P, PASSES, 2 * S], U8, "w4_w")
        gain_sb = held([P, ROW_TILES], F32, "gain_sb")
        w1_raw, w1_bf, w1_w, w1_sc = {}, {}, {}, {}
        h_bf, h_w, h_sc, h_acc = {}, {}, {}, {}
        v_w, v_sc, v2_w, f_sb = {}, {}, {}, {}
        for b in range(PASSES):
            for a in range(PASSES):
                w1_bf[b, a] = held([P, PACK, P, PACK], BF16, "w1_bf%d%d" % (b, a))
                w1_w[b, a] = held([P, KP], U32, "w1_w%d%d" % (b, a))
                w1_sc[b, a] = held([P, KP], U8, "w1_sc%d%d" % (b, a))
            for jh in range(S // HALF):
                h_bf[b, jh] = held([P, HALF, PACK], BF16, "h_bf%d%d" % (b, jh))
                h_sc[b, jh] = held([P, HALF], U8, "h_sc%d%d" % (b, jh))
        for jh in range(S // HALF):
            f_sb[jh] = held([P, ROW_TILES, HALF], F32, "f_sb%d" % jh)

        def load_tab(a, t0, t1):
            words = tab_words[a].rearrange("p t i -> p (t i)").bitcast(I32)
            nc.sync.dma_start(tab_w[a][:, t0:t1], words[:, t0:t1])

        def load_w1(b, a):
            w1_raw[b, a] = held([P, PACK, KP], F32, "w1_raw%d%d" % (b, a))
            block = w1[KP * a : KP * (a + 1), KP * b : KP * (b + 1)]
            nc.sync.dma_start(w1_raw[b, a][:], block.rearrange("(p t) c -> p t c", t=PACK))

        def entries(jh):
            return idx[:, jh * (HALF // LIST_ROWS) : (jh + 1) * (HALF // LIST_ROWS)]

        def gather_v(a, jh, reuses=None):
            v_w[a, jh] = held([P, HALF], U32, "v_w%d%d" % (a, jh), reuses)
            nc.vector.tensor_copy(v_w[a, jh][:], tab_w[a][:].bitcast(U32).indirect(entries(jh)))

        def gather_v_scales(jh):
            v_sc[jh] = held([P, HALF], U8, "v_sc%d" % jh)
            nc.vector.tensor_copy(v_sc[jh][:], tab_sc[:].indirect(entries(jh)))

        def gather_v2(a):
            v2_w[a] = held([P, S2], U32, "v2_w%d" % a)
            nc.vector.tensor_copy(v2_w[a][:], tab_w[a][:].bitcast(U32).indirect(idx2[:]))

        def cast_w1(b, a, u0, u1, on_vector):
            dst = w1_bf[b, a][:, u0:u1, :, :].rearrange("p u m t -> p m t u")
            src = w1_raw[b, a][:].rearrange("p t (m u) -> p m t u", u=PACK)[:, :, :, u0:u1]
            if on_vector:
                nc.vector.tensor_copy(dst, src)
            else:
                nc.scalar.activation(dst, src, ACT.Copy)

        def quantize_w1(b, a):
            nc.vector.quantize_mx(
                out=w1_w[b, a][:].bitcast(FP8X4),
                scales=w1_sc[b, a][:],
                in_=w1_bf[b, a][:].rearrange("p u m t -> p (u m t)"),
            )

        def h_pass(b, jh, c, a):
            if a == 0:
                h_acc[b, jh, c] = psum.tile([P, PACK, P], F32, name="h_acc", tag="bank")
            cols = slice(P * c, P * (c + 1))
            for u in range(PACK):
                rows = slice(P * u, P * (u + 1))
                nc.tensor.matmul_mx(
                    out=h_acc[b, jh, c][:, u, :],
                    lhsT=w1_w[b, a][:, rows].bitcast(FP8X4),
                    lhsT_scale=w1_sc[b, a][:, rows],
                    rhs=v_w[a, jh][:, cols].bitcast(FP8X4),
                    rhs_scale=v_sc[jh][PLANE_ROWS * a :, cols],
                    start=(a == 0 and u == 0),
                    stop=(a == PASSES - 1 and u == PACK - 1),
                )

        def h_finish(b, jh, c, on_vector=False):
            h_pass(b, jh, c, PASSES - 1)
            dst = h_bf[b, jh][:, P * c : P * (c + 1), :].rearrange("p (i l) u -> p i u l", l=2)
            src = h_acc[b, jh, c][:].rearrange("p u (i l) -> p i u l", l=2)
            if on_vector:
                nc.vector.tensor_scalar(dst, src, 0.0, None, ALU.max)
            else:
                nc.scalar.activation(dst, src, ACT.Relu)

        def quantize_h(b, jh, reuses=None):
            h_w[b, jh] = held([P, HALF], U32, "h_w%d%d" % (b, jh), reuses)
            nc.vector.quantize_mx(
                out=h_w[b, jh][:].bitcast(FP8X4),
                scales=h_sc[b, jh][:],
                in_=h_bf[b, jh][:].rearrange("p j u -> p (j u)"),
            )

        def v2_product(acc, mt, moving, moving_scales):
            rows = slice(P * mt, P * (mt + 1))
            for a in range(PASSES):
                nc.tensor.matmul_mx(
                    out=acc[:],
                    lhsT=v2_w[a][:, rows].bitcast(FP8X4),
                    lhsT_scale=v2_planes[a][:, rows],
                    rhs=moving(a),
                    rhs_scale=moving_scales(a),
                    start=(a == 0),
                    stop=(a == PASSES - 1),
                )

        def f_tile(jh, mt):
            acc = psum.tile([P, HALF], F32, name="f_acc", tag="bank")
            v2_product(
                acc,
                mt,
                lambda a: w4_w[:, a, 2 * HALF * jh : 2 * HALF * (jh + 1)].bitcast(FP4X4),
                lambda a: w4_sc[:, a, HALF * jh : HALF * (jh + 1)],
            )
            nc.scalar.activation(f_sb[jh][:, mt, :], acc[:], ACT.Copy)

        def e_tile(jh, mt):
            acc = psum.tile([P, HALF], F32, name="e_acc", tag="bank")
            v2_product(acc, mt, lambda b: h_w[b, jh][:].bitcast(FP8X4), lambda b: h_sc[b, jh][:])
            best = ring.tile([P, HALF], F32, name="best")
            res = ring.tile([P, HALF], F32, name="res")
            nc.vector.tensor_tensor(best[:], acc[:], f_sb[jh][:, mt, :], ALU.max)
            nc.vector.scalar_tensor_tensor(res[:], acc[:], gain_sb[:, mt : mt + 1], best[:], ALU.mult, ALU.add)
            nc.sync.dma_start(out[P * mt : P * (mt + 1), HALF * jh : HALF * (jh + 1)], res[:])

        load_tab(0, 0, T // 2)
        load_tab(0, T // 2, T)
        nc.sync.dma_start(idx[:], offs)
        nc.sync.dma_start(idx2[:], offs2)
        for q in QUADRANT_ORDER:
            nc.sync.dma_start(
                tab_sc[32 * q : 32 * q + PASSES * PLANE_ROWS, :].bitcast(I32),
                tab_scales[:, PLANE_ROWS * q : PLANE_ROWS * (q + 1), :].bitcast(I32),
            )
        load_w1(0, 0)
        load_w1(0, 1)
        load_w1(1, 0)
        load_tab(1, 0, T)

        for jh in range(S // HALF):
            gather_v(0, jh)
            gather_v_scales(jh)
        v2_sc = held([P, S2], U8, "v2_sc")
        nc.vector.tensor_copy(v2_sc[:], tab_sc[:].indirect(idx2[:]))
        nc.sync.dma_start(v2_sc1[0 : P - PLANE_ROWS, :].bitcast(I32), v2_sc[PLANE_ROWS:P, :].bitcast(I32))
        v2_planes = (v2_sc, v2_sc1)
        gather_v2(0)

        for q in QUADRANT_ORDER:
            nc.sync.dma_start(
                w4_sc[32 * q : 32 * q + PLANE_ROWS, :, :].bitcast(I32),
                w4_scales[:, PLANE_ROWS * q : PLANE_ROWS * (q + 1), :].rearrange("a r n -> r a n").bitcast(I32),
            )
        load_w1(1, 1)
        nc.sync.dma_start(w4_w[:].bitcast(I32), w4_words.rearrange("a p n -> p a n").bitcast(I32))
        with nc.allow_non_contiguous_dma(reason="one gain for each partition and row tile"):
            nc.sync.dma_start(gain_sb[:], gain.rearrange("(c p) -> p c", p=P))

        for a in range(PASSES):
            for u0 in range(0, PACK, 2):
                cast_w1(0, a, u0, u0 + 2, on_vector=False)
        quantize_w1(0, 0)
        cast_w1(1, 0, 0, 2, on_vector=True)
        cast_w1(1, 0, 2, PACK, on_vector=False)
        quantize_w1(0, 1)
        quantize_w1(1, 0)

        for jh in range(S // HALF):
            for c in range(CHUNKS):
                h_pass(0, jh, c, 0)
        gather_v(1, 0, reuses="w1_bf01")
        gather_v(1, 1, reuses="w1_bf10")
        gather_v2(1)
        for jh in range(S // HALF):
            for c in range(CHUNKS):
                h_finish(0, jh, c)

        cast_w1(1, 1, 0, PACK, on_vector=True)
        for c in range(CHUNKS):
            h_pass(1, 0, c, 0)
        quantize_w1(1, 1)
        quantize_h(0, 0, reuses="w1_bf11")
        quantize_h(0, 1, reuses="h_bf00")

        for c in range(CHUNKS):
            h_finish(1, 0, c, on_vector=(c == CHUNKS - 2))
        quantize_h(1, 0)

        f_tile(0, 0)
        f_tile(0, 1)
        for c in range(CHUNKS):
            if c < 2:
                e_tile(0, c)
            h_pass(1, 1, c, 0)
            h_finish(1, 1, c)
        quantize_h(1, 1)
        for tile_no in range(2, (S // HALF) * ROW_TILES):
            jh, mt = divmod(tile_no, ROW_TILES)
            f_tile(jh, mt)
            e_tile(jh, mt)
